import numpy as np
import ml_dtypes

BF16 = ml_dtypes.bfloat16


def bf(x):
    return np.asarray(x, np.float32).astype(BF16)


def f32(x):
    return np.asarray(x, np.float32)


def f64(x):
    return np.asarray(x).astype(np.float64)


def striped(idx):
    return np.tile(idx.reshape(-1, 16).T, (8, 1))


S, K, M, N, E, Q = 512, 256, 256, 384, 2, 192


def setup_inputs():
    return {"base": bf(np.random.standard_normal((M, S))), "x": bf(np.random.standard_normal((K, N))), "w": bf(np.random.standard_normal((E, K, M)) / np.sqrt(K)), "offs": striped(np.random.permutation(S)[:N])}


def reference(base, x, w, offs):
    idx = offs[:16].T.reshape(-1)
    z = f64(base).copy()
    for e in range(E):
        z[:, idx[e * Q : (e + 1) * Q]] += f64(w)[e].T @ f64(x)[:, e * Q : (e + 1) * Q]
    return z

@@ -1,0 +1,60 @@
+import concourse.mybir as mybir
+from concourse.masks import make_identity
+
+BF16, F32, U16 = mybir.dt.bfloat16, mybir.dt.float32, mybir.dt.uint16
+
+P = 128
+S = 512
+K = 256
+M = 256
+N = 384
+E = 2
+Q = N // E
+KB = K // P
+MB = M // P
+QC = Q // 16
+
+FLOPS = 2 * K * M * N
+
+
+def tile_scatter_matmul_kernel(tc, base, x, w, offs, out):
+    nc = tc.nc
+    with (
+        tc.tile_pool(name="held", bufs=1) as held,
+        tc.psum_pool(name="banks", bufs=1) as banks,
+    ):
+        offsets = held.tile([P, N // 16], U16, name="offsets")
+        nc.sync.dma_start(offsets[:], offs)
+
+        base_sb = [held.tile([P, S], BF16, name=f"base{mb}") for mb in range(MB)]
+        nc.sync.dma_start(base_sb[0][:], base[0:P, :])
+        nc.scalar.dma_start(base_sb[1][:], base[P : 2 * P, :])
+
+        x_sb = held.tile([P, KB, N], BF16, name="x_sb")
+        nc.sync.dma_start(x_sb[:], x.rearrange("(kb p) n -> p kb n", p=P))
+        w_sb = [held.tile([P, KB, M], BF16, name=f"w{e}") for e in range(E)]
+        for e in range(E):
+            nc.scalar.dma_start(w_sb[e][:], w[e].rearrange("(kb p) m -> p kb m", p=P))
+
+        ident = held.tile([P, P], BF16, name="ident")
+        make_identity(nc, ident[:])
+
+        windows = [banks.tile([P, S], F32, name=f"window{mb}") for mb in range(MB)]
+        for mb in range(MB):
+            nc.tensor.matmul(windows[mb][:], ident[:], base_sb[mb][:], start=True, stop=False)
+
+        for mb in range(MB):
+            for e in range(E):
+                for kb in range(KB):
+                    nc.tensor.matmul(
+                        windows[mb][:].indirect(offsets[:, e * QC : (e + 1) * QC]),
+                        w_sb[e][:, kb, mb * P : (mb + 1) * P],
+                        x_sb[:, kb, e * Q : (e + 1) * Q],
+                        start=False,
+                        stop=(e == E - 1 and kb == KB - 1),
+                    )
+
+        for mb in range(MB):
+            z_sb = held.tile([P, S], F32, name=f"z{mb}")
+            nc.vector.tensor_copy(z_sb[:], windows[mb][:])
+            nc.sync.dma_start(out[mb * P : (mb + 1) * P, :], z_sb[:])

@@ -13,6 +13,7 @@ Q = N // E
 KB = K // P
 MB = M // P
 QC = Q // 16
+WARM = 14
 
 FLOPS = 2 * K * M * N
 
@@ -38,6 +39,12 @@ def tile_scatter_matmul_kernel(tc, base, x, w, offs, out):
 
         ident = held.tile([P, P], BF16, name="ident")
         make_identity(nc, ident[:])
+
+        zeros = held.tile([P, P], BF16, name="zeros")
+        nc.vector.memset(zeros[:], 0.0)
+        unread = banks.tile([P, P], F32, name="unread")
+        for i in range(WARM):
+            nc.tensor.matmul(unread[:], zeros[:], zeros[:], start=True, stop=True)
 
         windows = [banks.tile([P, S], F32, name=f"window{mb}") for mb in range(MB)]
         for mb in range(MB):

@@ -24,18 +24,20 @@ def tile_scatter_matmul_kernel(tc, base, x, w, offs, out):
         tc.tile_pool(name="held", bufs=1) as held,
         tc.psum_pool(name="banks", bufs=1) as banks,
     ):
-        offsets = held.tile([P, N // 16], U16, name="offsets")
-        nc.sync.dma_start(offsets[:], offs)
-
         base_sb = [held.tile([P, S], BF16, name=f"base{mb}") for mb in range(MB)]
         nc.sync.dma_start(base_sb[0][:], base[0:P, :])
         nc.scalar.dma_start(base_sb[1][:], base[P : 2 * P, :])
 
-        x_sb = held.tile([P, KB, N], BF16, name="x_sb")
-        nc.sync.dma_start(x_sb[:], x.rearrange("(kb p) n -> p kb n", p=P))
+        offsets = held.tile([P, N // 16], U16, name="offsets")
+        nc.sync.dma_start(offsets[:], offs)
+
+        x_sb = [held.tile([P, KB, Q], BF16, name=f"x{e}") for e in range(E)]
         w_sb = [held.tile([P, KB, M], BF16, name=f"w{e}") for e in range(E)]
         for e in range(E):
-            nc.scalar.dma_start(w_sb[e][:], w[e].rearrange("(kb p) m -> p kb m", p=P))
+            nc.sync.dma_start(
+                x_sb[e][:], x[:, e * Q : (e + 1) * Q].rearrange("(p kb) q -> p kb q", kb=KB)
+            )
+            nc.scalar.dma_start(w_sb[e][:], w[e].rearrange("(p kb) m -> p kb m", kb=KB))
 
         ident = held.tile([P, P], BF16, name="ident")
         make_identity(nc, ident[:])
@@ -50,18 +52,19 @@ def tile_scatter_matmul_kernel(tc, base, x, w, offs, out):
         for mb in range(MB):
             nc.tensor.matmul(windows[mb][:], ident[:], base_sb[mb][:], start=True, stop=False)
 
-        for mb in range(MB):
-            for e in range(E):
+        for e in range(E):
+            for mb in range(MB):
                 for kb in range(KB):
                     nc.tensor.matmul(
                         windows[mb][:].indirect(offsets[:, e * QC : (e + 1) * QC]),
                         w_sb[e][:, kb, mb * P : (mb + 1) * P],
-                        x_sb[:, kb, e * Q : (e + 1) * Q],
+                        x_sb[e][:, kb, :],
                         start=False,
                         stop=(e == E - 1 and kb == KB - 1),
                     )
 
-        for mb in range(MB):
-            z_sb = held.tile([P, S], F32, name=f"z{mb}")
-            nc.vector.tensor_copy(z_sb[:], windows[mb][:])
-            nc.sync.dma_start(out[mb * P : (mb + 1) * P, :], z_sb[:])
+        z_sb = [held.tile([P, S], F32, name=f"z{mb}") for mb in range(MB)]
+        nc.vector.tensor_copy(z_sb[0][:], windows[0][:])
+        nc.sync.dma_start(out[0:P, :], z_sb[0][:])
+        nc.scalar.copy(z_sb[1][:], windows[1][:])
+        nc.scalar.dma_start(out[P : 2 * P, :], z_sb[1][:])

@@ -26,7 +26,7 @@ def tile_scatter_matmul_kernel(tc, base, x, w, offs, out):
     ):
         base_sb = [held.tile([P, S], BF16, name=f"base{mb}") for mb in range(MB)]
         nc.sync.dma_start(base_sb[0][:], base[0:P, :])
-        nc.scalar.dma_start(base_sb[1][:], base[P : 2 * P, :])
+        nc.sync.dma_start(base_sb[1][:], base[P : 2 * P, :])
 
         offsets = held.tile([P, N // 16], U16, name="offsets")
         nc.sync.dma_start(offsets[:], offs)
@@ -37,7 +37,7 @@ def tile_scatter_matmul_kernel(tc, base, x, w, offs, out):
             nc.sync.dma_start(
                 x_sb[e][:], x[:, e * Q : (e + 1) * Q].rearrange("(p kb) q -> p kb q", kb=KB)
             )
-            nc.scalar.dma_start(w_sb[e][:], w[e].rearrange("(p kb) m -> p kb m", kb=KB))
+            nc.sync.dma_start(w_sb[e][:], w[e].rearrange("(p kb) m -> p kb m", kb=KB))
 
         ident = held.tile([P, P], BF16, name="ident")
         make_identity(nc, ident[:])

@@ -32,12 +32,13 @@ def tile_scatter_matmul_kernel(tc, base, x, w, offs, out):
         nc.sync.dma_start(offsets[:], offs)
 
         x_sb = [held.tile([P, KB, Q], BF16, name=f"x{e}") for e in range(E)]
-        w_sb = [held.tile([P, KB, M], BF16, name=f"w{e}") for e in range(E)]
+        w_sb = [[held.tile([P, M], BF16, name=f"w{e}_{kb}") for kb in range(KB)] for e in range(E)]
         for e in range(E):
             nc.sync.dma_start(
-                x_sb[e][:], x[:, e * Q : (e + 1) * Q].rearrange("(p kb) q -> p kb q", kb=KB)
+                x_sb[e][:], x[:, e * Q : (e + 1) * Q].rearrange("(kb p) q -> p kb q", p=P)
             )
-            nc.sync.dma_start(w_sb[e][:], w[e].rearrange("(p kb) m -> p kb m", kb=KB))
+            for kb in range(KB):
+                nc.sync.dma_start(w_sb[e][kb][:], w[e, kb * P : (kb + 1) * P, :])
 
         ident = held.tile([P, P], BF16, name="ident")
         make_identity(nc, ident[:])
@@ -53,11 +54,11 @@ def tile_scatter_matmul_kernel(tc, base, x, w, offs, out):
             nc.tensor.matmul(windows[mb][:], ident[:], base_sb[mb][:], start=True, stop=False)
 
         for e in range(E):
-            for mb in range(MB):
-                for kb in range(KB):
+            for kb in range(KB):
+                for mb in range(MB):
                     nc.tensor.matmul(
                         windows[mb][:].indirect(offsets[:, e * QC : (e + 1) * QC]),
-                        w_sb[e][:, kb, mb * P : (mb + 1) * P],
+                        w_sb[e][kb][:, mb * P : (mb + 1) * P],
                         x_sb[e][:, kb, :],
                         start=False,
                         stop=(e == E - 1 and kb == KB - 1),

@@ -31,13 +31,11 @@ def tile_scatter_matmul_kernel(tc, base, x, w, offs, out):
         offsets = held.tile([P, N // 16], U16, name="offsets")
         nc.sync.dma_start(offsets[:], offs)
 
-        x_sb = [held.tile([P, KB, Q], BF16, name=f"x{e}") for e in range(E)]
+        x_sb = [[held.tile([P, Q], BF16, name=f"x{e}_{kb}") for kb in range(KB)] for e in range(E)]
         w_sb = [[held.tile([P, M], BF16, name=f"w{e}_{kb}") for kb in range(KB)] for e in range(E)]
         for e in range(E):
-            nc.sync.dma_start(
-                x_sb[e][:], x[:, e * Q : (e + 1) * Q].rearrange("(kb p) q -> p kb q", p=P)
-            )
             for kb in range(KB):
+                nc.sync.dma_start(x_sb[e][kb][:], x[kb * P : (kb + 1) * P, e * Q : (e + 1) * Q])
                 nc.sync.dma_start(w_sb[e][kb][:], w[e, kb * P : (kb + 1) * P, :])
 
         ident = held.tile([P, P], BF16, name="ident")
@@ -59,7 +57,7 @@ def tile_scatter_matmul_kernel(tc, base, x, w, offs, out):
                     nc.tensor.matmul(
                         windows[mb][:].indirect(offsets[:, e * QC : (e + 1) * QC]),
                         w_sb[e][kb][:, mb * P : (mb + 1) * P],
-                        x_sb[e][:, kb, :],
+                        x_sb[e][kb][:],
                         start=False,
                         stop=(e == E - 1 and kb == KB - 1),
                     )

@@ -13,7 +13,7 @@ Q = N // E
 KB = K // P
 MB = M // P
 QC = Q // 16
-WARM = 14
+WARM = 9
 
 FLOPS = 2 * K * M * N
 

@@ -13,7 +13,7 @@ Q = N // E
 KB = K // P
 MB = M // P
 QC = Q // 16
-WARM = 9
+WARM = 2
 
 FLOPS = 2 * K * M * N
 
@@ -43,9 +43,15 @@ def tile_scatter_matmul_kernel(tc, base, x, w, offs, out):
 
         zeros = held.tile([P, P], BF16, name="zeros")
         nc.vector.memset(zeros[:], 0.0)
-        unread = banks.tile([P, P], F32, name="unread")
+        unread = banks.tile([P, S // P, P], F32, name="unread")
         for i in range(WARM):
-            nc.tensor.matmul(unread[:], zeros[:], zeros[:], start=True, stop=True)
+            nc.tensor.matmul(
+                unread[:],
+                zeros[:],
+                zeros[:].unsqueeze(1).to_broadcast([P, S // P, P]),
+                start=True,
+                stop=True,
+            )
 
         windows = [banks.tile([P, S], F32, name=f"window{mb}") for mb in range(MB)]
         for mb in range(MB):

@@ -13,6 +13,7 @@ Q = N // E
 KB = K // P
 MB = M // P
 QC = Q // 16
+CUT = 256
 WARM = 2
 
 FLOPS = 2 * K * M * N
@@ -31,11 +32,11 @@ def tile_scatter_matmul_kernel(tc, base, x, w, offs, out):
         offsets = held.tile([P, N // 16], U16, name="offsets")
         nc.sync.dma_start(offsets[:], offs)
 
-        x_sb = [[held.tile([P, Q], BF16, name=f"x{e}_{kb}") for kb in range(KB)] for e in range(E)]
+        x_sb = [held.tile([P, N], BF16, name=f"x{kb}") for kb in range(KB)]
         w_sb = [[held.tile([P, M], BF16, name=f"w{e}_{kb}") for kb in range(KB)] for e in range(E)]
-        for e in range(E):
+        for e, columns in enumerate([slice(0, CUT), slice(CUT, N)]):
             for kb in range(KB):
-                nc.sync.dma_start(x_sb[e][kb][:], x[kb * P : (kb + 1) * P, e * Q : (e + 1) * Q])
+                nc.sync.dma_start(x_sb[kb][:, columns], x[kb * P : (kb + 1) * P, columns])
                 nc.sync.dma_start(w_sb[e][kb][:], w[e, kb * P : (kb + 1) * P, :])
 
         ident = held.tile([P, P], BF16, name="ident")
@@ -63,7 +64,7 @@ def tile_scatter_matmul_kernel(tc, base, x, w, offs, out):
                     nc.tensor.matmul(
                         windows[mb][:].indirect(offsets[:, e * QC : (e + 1) * QC]),
                         w_sb[e][kb][:, mb * P : (mb + 1) * P],
-                        x_sb[e][kb][:],
+                        x_sb[kb][:, e * Q : (e + 1) * Q],
                         start=False,
                         stop=(e == E - 1 and kb == KB - 1),
                     )

@@ -14,6 +14,7 @@ KB = K // P
 MB = M // P
 QC = Q // 16
 CUT = 256
+Z = 32
 WARM = 2
 
 FLOPS = 2 * K * M * N
@@ -36,20 +37,25 @@ def tile_scatter_matmul_kernel(tc, base, x, w, offs, out):
         w_sb = [[held.tile([P, M], BF16, name=f"w{e}_{kb}") for kb in range(KB)] for e in range(E)]
         for e, columns in enumerate([slice(0, CUT), slice(CUT, N)]):
             for kb in range(KB):
-                nc.sync.dma_start(x_sb[kb][:, columns], x[kb * P : (kb + 1) * P, columns])
-                nc.sync.dma_start(w_sb[e][kb][:], w[e, kb * P : (kb + 1) * P, :])
+                rows = slice(kb * P, (kb + 1) * P)
+                nc.sync.dma_start(x_sb[kb][:, columns], x[rows, columns])
+                weight_loads = MB if e == 0 and kb == 0 else 1
+                width = M // weight_loads
+                for i in range(weight_loads):
+                    features = slice(i * width, (i + 1) * width)
+                    nc.sync.dma_start(w_sb[e][kb][:, features], w[e, rows, features])
 
         ident = held.tile([P, P], BF16, name="ident")
         make_identity(nc, ident[:])
 
-        zeros = held.tile([P, P], BF16, name="zeros")
+        zeros = held.tile([P, Z], BF16, name="zeros")
         nc.vector.memset(zeros[:], 0.0)
-        unread = banks.tile([P, S // P, P], F32, name="unread")
+        unread = banks.tile([Z, S // Z, Z], F32, name="unread")
         for i in range(WARM):
             nc.tensor.matmul(
                 unread[:],
                 zeros[:],
-                zeros[:].unsqueeze(1).to_broadcast([P, S // P, P]),
+                zeros[:].unsqueeze(1).to_broadcast([P, S // Z, Z]),
                 start=True,
                 stop=True,
             )
@@ -71,6 +77,6 @@ def tile_scatter_matmul_kernel(tc, base, x, w, offs, out):
 
         z_sb = [held.tile([P, S], F32, name=f"z{mb}") for mb in range(MB)]
         nc.vector.tensor_copy(z_sb[0][:], windows[0][:])
-        nc.sync.dma_start(out[0:P, :], z_sb[0][:])
         nc.scalar.copy(z_sb[1][:], windows[1][:])
-        nc.scalar.dma_start(out[P : 2 * P, :], z_sb[1][:])
+        for mb in range(MB):
+            nc.scalar.dma_start(out[mb * P : (mb + 1) * P, :], z_sb[mb][:])

@@ -37,13 +37,8 @@ def tile_scatter_matmul_kernel(tc, base, x, w, offs, out):
         w_sb = [[held.tile([P, M], BF16, name=f"w{e}_{kb}") for kb in range(KB)] for e in range(E)]
         for e, columns in enumerate([slice(0, CUT), slice(CUT, N)]):
             for kb in range(KB):
-                rows = slice(kb * P, (kb + 1) * P)
-                nc.sync.dma_start(x_sb[kb][:, columns], x[rows, columns])
-                weight_loads = MB if e == 0 and kb == 0 else 1
-                width = M // weight_loads
-                for i in range(weight_loads):
-                    features = slice(i * width, (i + 1) * width)
-                    nc.sync.dma_start(w_sb[e][kb][:, features], w[e, rows, features])
+                nc.sync.dma_start(x_sb[kb][:, columns], x[kb * P : (kb + 1) * P, columns])
+                nc.sync.dma_start(w_sb[e][kb][:], w[e, kb * P : (kb + 1) * P, :])
 
         ident = held.tile([P, P], BF16, name="ident")
         make_identity(nc, ident[:])

import concourse.mybir as mybir
from concourse.masks import make_identity

BF16, F32, U16 = mybir.dt.bfloat16, mybir.dt.float32, mybir.dt.uint16

P = 128
S = 512
K = 256
M = 256
N = 384
E = 2
Q = N // E
KB = K // P
MB = M // P
QC = Q // 16
CUT = 256
Z = 32
WARM = 2

FLOPS = 2 * K * M * N


def tile_scatter_matmul_kernel(tc, base, x, w, offs, out):
    nc = tc.nc
    with (
        tc.tile_pool(name="held", bufs=1) as held,
        tc.psum_pool(name="banks", bufs=1) as banks,
    ):
        base_sb = [held.tile([P, S], BF16, name=f"base{mb}") for mb in range(MB)]
        nc.sync.dma_start(base_sb[0][:], base[0:P, :])
        nc.sync.dma_start(base_sb[1][:], base[P : 2 * P, :])

        offsets = held.tile([P, N // 16], U16, name="offsets")
        nc.sync.dma_start(offsets[:], offs)

        x_sb = [held.tile([P, N], BF16, name=f"x{kb}") for kb in range(KB)]
        w_sb = [[held.tile([P, M], BF16, name=f"w{e}_{kb}") for kb in range(KB)] for e in range(E)]
        for e, columns in enumerate([slice(0, CUT), slice(CUT, N)]):
            for kb in range(KB):
                nc.sync.dma_start(x_sb[kb][:, columns], x[kb * P : (kb + 1) * P, columns])
                nc.sync.dma_start(w_sb[e][kb][:], w[e, kb * P : (kb + 1) * P, :])

        ident = held.tile([P, P], BF16, name="ident")
        make_identity(nc, ident[:])

        zeros = held.tile([P, Z], BF16, name="zeros")
        nc.vector.memset(zeros[:], 0.0)
        unread = banks.tile([Z, S // Z, Z], F32, name="unread")
        for i in range(WARM):
            nc.tensor.matmul(
                unread[:],
                zeros[:],
                zeros[:].unsqueeze(1).to_broadcast([P, S // Z, Z]),
                start=True,
                stop=True,
            )

        windows = [banks.tile([P, S], F32, name=f"window{mb}") for mb in range(MB)]
        for mb in range(MB):
            nc.tensor.matmul(windows[mb][:], ident[:], base_sb[mb][:], start=True, stop=False)

        for e in range(E):
            for kb in range(KB):
                for mb in range(MB):
                    nc.tensor.matmul(
                        windows[mb][:].indirect(offsets[:, e * QC : (e + 1) * QC]),
                        w_sb[e][kb][:, mb * P : (mb + 1) * P],
                        x_sb[kb][:, e * Q : (e + 1) * Q],
                        start=False,
                        stop=(e == E - 1 and kb == KB - 1),
                    )

        z_sb = [held.tile([P, S], F32, name=f"z{mb}") for mb in range(MB)]
        nc.vector.tensor_copy(z_sb[0][:], windows[0][:])
        nc.scalar.copy(z_sb[1][:], windows[1][:])
        for mb in range(MB):
            nc.scalar.dma_start(out[mb * P : (mb + 1) * P, :], z_sb[mb][:])
